import numpy as np
import ml_dtypes


def mxq(x, axis, fmt="e4m3"):
    dtype, down = {"e4m3": (ml_dtypes.float8_e4m3fn, 7), "e5m2": (ml_dtypes.float8_e5m2, 14)}[fmt]
    v = np.moveaxis(np.asarray(x, np.float32).astype(ml_dtypes.bfloat16).astype(np.float64), axis, -1)
    blocks = v.reshape(v.shape[:-1] + (-1, 32))
    amax = np.abs(blocks).max(-1, keepdims=True)
    byte = np.maximum(np.where(amax > 0, np.frexp(amax)[1] - 1 + 127, 0) - down, 1)
    scale = np.exp2(byte - 127.0)
    codes = (blocks / scale).astype(np.float32).astype(dtype).astype(np.float64)
    return np.moveaxis((codes * scale).reshape(v.shape), -1, axis)


WIDE = False


def mx_kscale(k):
    if not WIDE:
        return np.ones(k)
    levels = np.array([10, -10, 5, -5, 0])
    if k % 512:
        return np.exp2(np.random.permutation(np.resize(levels, k // 32))).repeat(32)
    a = np.empty((k // 512, 16))
    for p in range(k // 512):
        a[p, :8] = np.random.permutation(np.resize(levels, 8))
        for g in range(8):
            far = levels[np.abs(levels - a[p, g]) >= 10]
            a[p, g + 8] = far[np.random.randint(len(far))]
    return np.exp2(a.ravel()).repeat(32)


def f64(x):
    return np.asarray(x).astype(np.float64)


def striped(idx):
    return np.tile(np.asarray(idx).reshape(-1, 16).T, (8, 1)).astype(np.uint16)


def unstriped(offs):
    return offs[:16].T.reshape(-1).astype(np.int64)


E2M1 = np.array([0.0, 0.5, 1.0, 1.5, 2.0, 3.0, 4.0, 6.0, -0.0, -0.5, -1.0, -1.5, -2.0, -3.0, -4.0, -6.0])


def pack_weight(w, fmt):
    k, n = w.shape
    w = f64(np.asarray(w, np.float32).astype(ml_dtypes.bfloat16)).reshape(k // 32, 32, n)
    amax = np.abs(w).max(1)
    if fmt == "e4m3":
        byte = np.frexp(amax)[1] - 1 + 127 - 7
    else:
        mant, ex = np.frexp(amax / 6.0)
        byte = np.where(mant > 0.5, ex, ex - 1) + 127
    byte = np.clip(np.where(amax > 0, byte, 1), 1, 254)
    scaled = (w * np.exp2(127.0 - byte)[:, None, :]).reshape(k, n).astype(np.float32)
    by_word = np.ascontiguousarray(scaled.reshape(k // 512, 128, 4, n).transpose(0, 1, 3, 2))
    if fmt == "e4m3":
        words = by_word.astype(ml_dtypes.float8_e4m3fn).view(np.uint8)
    else:
        c = by_word.astype(ml_dtypes.float4_e2m1fn).view(np.uint8) & 0xF
        words = (c[..., 0::2] | (c[..., 1::2] << 4)).reshape(k // 512, 128, 2 * n)
    return np.ascontiguousarray(words), np.ascontiguousarray(byte.astype(np.uint8).reshape(k // 512, 16, n))


def unpack_weight(words, scales, fmt):
    g, _, n = scales.shape
    words = np.ascontiguousarray(words).reshape(g, 128, n, -1)
    if fmt == "e4m3":
        vals = words.view(ml_dtypes.float8_e4m3fn).astype(np.float64)
    else:
        nib = np.empty((g, 128, n, 4), np.uint8)
        nib[..., 0::2] = words & 0xF
        nib[..., 1::2] = words >> 4
        vals = E2M1[nib]
    vals = vals * np.repeat(np.exp2(scales.astype(np.float64) - 127.0), 8, axis=1)[..., None]
    return vals.transpose(0, 1, 3, 2).reshape(g * 512, n)


D, E, T, I, Q, G = 512, 512, 1024, 256, 512, 16


def setup_inputs():
    n = np.random.standard_normal
    idx = np.random.permutation(T)[:I]
    fd = mx_kscale(D)
    fq = mx_kscale(Q)
    keysp = pack_weight(n((D, T)) / fd[:, None], "e2m1")
    return {
        "query": (n((D, Q)) * 0.5 / np.sqrt(D) * fd[:, None]).astype(np.float32),
        "qs": (np.random.uniform(8.0, 32.0, (Q, 1)) * fq[:, None]).astype(np.float32),
        "grows": (n((Q, E)) / fq[:, None]).astype(np.float32),
        "vals": (n((E, T))).astype(np.float32),
        "keys_words": keysp[0],
        "keys_scales": keysp[1],
        "share": (np.random.uniform(0.4, 1.0, (E, 1))).astype(np.float32),
        "pre": (np.random.uniform(0.6, 1.6, (1, I))).astype(np.float32),
        "sg": (np.random.uniform(0.5, 2.0, (1, I))).astype(np.float32),
        "old": (n((E, T)) * 1.0).astype(np.float32),
        "fade": (np.random.uniform(0.5, 1.0, (1, T))).astype(np.float32),
        "offs": striped(idx),
    }


def reference(query, qs, grows, vals, keys_words, keys_scales, share, pre, sg, old, fade, offs):
    idx = unstriped(offs)
    keysu = unpack_weight(keys_words, keys_scales, "e2m1")
    queryq = mxq(f64(query), 0, "e4m3")
    keysidxg = keysu[:, idx]
    a = queryq.T @ keysidxg
    p = np.exp(a - np.max(a, axis=1, keepdims=True))
    w = p * f64(qs) / np.sum(p, axis=1, keepdims=True)
    growsq = mxq(f64(grows), 0, "e4m3")
    wq = mxq(w, 0, "e4m3")
    c0 = growsq.T @ wq
    x1 = f64(vals)[:, idx] * f64(pre)
    m1 = x1.reshape(E, G, I // G).mean(axis=2)
    mr = np.repeat(m1, I // G, axis=1)
    x2 = x1 - mr * f64(share)
    vp = np.tanh(x2)
    dx2 = c0 * (1.0 - np.square(vp))
    dmr = dx2 * (-1.0) * f64(share)
    dm1 = dmr.reshape(E, G, I // G).sum(axis=2)
    e1 = dm1 / 16.0
    r1 = np.repeat(e1, I // G, axis=1)
    dx1 = dx2 + r1
    gs = dx1 * f64(sg)
    gf = np.zeros((E, T))
    gf[:, idx] = gs
    y = f64(old) * f64(fade) + gf
    return y

@@ -1,0 +1,292 @@
+from contextlib import ExitStack
+
+import concourse.mybir as mybir
+from concourse.masks import make_identity
+
+D, E, T, I, Q, G = 512, 512, 1024, 256, 512, 16
+FLOPS = 2 * D * Q * I + 2 * Q * E * I
+
+F32 = mybir.dt.float32
+BF16 = mybir.dt.bfloat16
+I32 = mybir.dt.int32
+U32 = mybir.dt.uint32
+U16 = mybir.dt.uint16
+U8 = mybir.dt.uint8
+FP8X4 = mybir.dt.float8_e4m3fn_x4
+FP4X4 = mybir.dt.float4_e2m1fn_x4
+ALU = mybir.AluOpType
+ACT = mybir.ActivationFunctionType
+AX = mybir.AxisListType
+
+P = 128
+PACK = 4
+PAGE = I // G
+NE = E // P
+NB = T // P
+BANK = {name: 2048 * n for n, name in enumerate(("s0", "s1", "c0", "c1", "x0", "x1", "y0", "y1"))}
+
+
+def tile_attend_bvpagecentred_s_kernel(tc, query, qs, grows, vals, keys_words, keys_scales, share, pre, sg, old, fade, offs, out):
+    nc = tc.nc
+    with ExitStack() as ctx:
+        keep = ctx.enter_context(tc.tile_pool(name="keep", bufs=1))
+        work = ctx.enter_context(tc.tile_pool(name="work", bufs=2))
+        outp = ctx.enter_context(tc.tile_pool(name="outp", bufs=8))
+        ring = ctx.enter_context(tc.tile_pool(name="ring", bufs=1))
+        turns = ctx.enter_context(tc.tile_pool(name="turns", bufs=1))
+        psum = ctx.enter_context(tc.psum_pool(name="psum", bufs=1))
+
+        offsets = keep.tile([P, I // 16], U16, name="offsets")
+        key_words = keep.tile([P, T], U16, name="key_words")
+        key_scales = keep.tile([P, T], U8, name="key_scales")
+        rows = keep.tile([P, P], F32, name="rows")
+        ident = keep.tile([P, P], F32, name="ident")
+        warm = keep.tile([P, 1], F32, name="warm")
+        warm_out = keep.tile([P, 1], F32, name="warm_out")
+
+        nc.gpsimd.memset(rows[:], 0.0)
+        make_identity(nc, ident[:])
+        nc.vector.memset(key_scales[:].bitcast(I32), 0)
+        nc.vector.memset(warm[:], 0.0)
+        nc.scalar.activation(warm_out[:], warm[:], ACT.Exp)
+
+        slot_cols = [turns.tile([P, 2], F32, name="pre_cols", offset=18432, align_bytes=64), keep.tile([P, 2], F32, name="sg_cols")]
+        share_cols = keep.tile([P, NE], F32, name="share_cols")
+        qs_cols = keep.tile([P, PACK], F32, name="qs_cols")
+        q_raw = [ring.tile([P, PACK, Q // 2], F32, name=f"q_raw{h}", offset=4096 * h) for h in range(2)]
+
+        def load_query(h):
+            nc.sync.dma_start(q_raw[h][:], query.rearrange("(p j) q -> p j q", j=PACK)[:, :, 256 * h : 256 * h + 256])
+
+        nc.sync.dma_start(offsets[:], offs)
+        nc.sync.dma_start(slot_cols[0][:], pre.rearrange("o (p c) -> p (o c)", c=2))
+        load_query(0)
+        nc.sync.dma_start(key_words[:].bitcast(I32), keys_words[0].bitcast(I32))
+        load_query(1)
+        for quad in range(4):
+            nc.scalar.dma_start(key_scales[32 * quad : 32 * quad + 4, :].bitcast(I32), keys_scales[0, 4 * quad : 4 * quad + 4, :].bitcast(I32))
+        nc.sync.dma_start(share_cols[:], share.rearrange("(j p) o -> p (j o)", p=P), allow_slow_non_contiguous=True)
+        nc.sync.dma_start(qs_cols[:], qs.rearrange("(p r) o -> p (r o)", r=PACK))
+
+        v_pool, g_raw, old_raw = {}, {}, {}
+
+        def load_vals(j):
+            v_pool[j] = ring.tile([P, T], F32, name=f"v_pool{j}", offset=4096 * (3, 4, 0, 1)[j])
+            nc.sync.dma_start(v_pool[j][:], vals[P * j : P * (j + 1), :])
+
+        def load_grows(h):
+            g_raw[h] = ring.tile([P, PACK, E // 2], F32, name=f"g_raw{h}", offset=4096 * 2)
+            nc.sync.dma_start(g_raw[h][:], grows.rearrange("(p r) e -> p r e", r=PACK)[:, :, 256 * h : 256 * h + 256])
+
+        load_grows(0)
+        load_vals(0)
+        nc.sync.dma_start(slot_cols[1][:], sg.rearrange("o (p c) -> p (o c)", c=2))
+        nc.sync.dma_start(rows[0:8, :], fade.rearrange("o (b p) -> (o b) p", p=P))
+        load_vals(1)
+        load_vals(2)
+        load_vals(3)
+        load_grows(1)
+
+        gf = {}
+        for j in (0, 1, 3):
+            gf[j] = keep.tile([P, T], F32, name=f"gf{j}")
+            nc.vector.memset(gf[j][:], 0.0)
+
+        nshare = keep.tile([P, NE], F32, name="nshare")
+        nc.gpsimd.tensor_scalar(nshare[:], share_cols[:], -1.0 / PAGE, 0.0, ALU.mult, ALU.add)
+        pre_row = keep.tile([P, I], F32, name="pre_row")
+        nsg_row = keep.tile([P, I], F32, name="nsg_row")
+        for c in range(2):
+            spread = psum.tile([P, P], F32, name=f"pre_spread{c}", offset=BANK[f"s{c}"])
+            nc.tensor.transpose(spread[:], slot_cols[0][:, c : c + 1].to_broadcast([P, P]), ident[:])
+            nc.scalar.copy(pre_row[:, c::2], spread[:])
+
+        k_codes = keep.tile([P, I], U16, name="k_codes", align_bytes=64)
+        k_scales = keep.tile([P, I], U8, name="k_scales", align_bytes=64)
+        nc.vector.tensor_copy(k_codes[:], key_words[:].indirect(offsets[:]))
+        nc.vector.tensor_copy(k_scales[:], key_scales[:].indirect(offsets[:]))
+
+        q_woven = turns.tile([P, PACK, P, PACK], BF16, name="q_woven", offset=18432, align_bytes=64)
+
+        def weave_q(eng, h, s0, s1):
+            dst = q_woven[:, :, 64 * h + s0 : 64 * h + s1, :].rearrange("p r s j -> p s j r")
+            src = q_raw[h][:, :, 4 * s0 : 4 * s1].rearrange("p j (s r) -> p s j r", r=PACK)
+            if eng == "v":
+                nc.vector.tensor_copy(dst, src)
+            else:
+                nc.scalar.copy(dst, src)
+
+        weave_q("v", 0, 0, 64)
+        weave_q("v", 1, 0, 40)
+        weave_q("s", 1, 40, 64)
+        q_codes = turns.tile([P, Q], U32, name="q_codes", offset=3072, align_bytes=64)
+        q_scales = keep.tile([P, Q], U8, name="q_scales", align_bytes=64)
+        for b in range(2):
+            nc.vector.quantize_mx(
+                out=q_codes[:, 256 * b : 256 * b + 256].bitcast(FP8X4),
+                scales=q_scales[:, 256 * b : 256 * b + 256],
+                in_=q_woven[:, 2 * b : 2 * b + 2, :, :].rearrange("p r s j -> p (r s j)"),
+            )
+        gf[2] = turns.tile([P, T], F32, name="gf2", offset=18432 + 2048, align_bytes=64)
+        nc.vector.memset(gf[2][:], 0.0)
+        score = [psum.tile([P, 2, I], F32, name=f"score{b}", offset=BANK[f"s{b}"]) for b in range(2)]
+        for r in range(PACK):
+            nc.tensor.matmul_mx(
+                out=score[r // 2][:, r % 2, :],
+                lhsT=q_codes[:, P * r : P * (r + 1)].bitcast(FP8X4),
+                lhsT_scale=q_scales[:, P * r : P * (r + 1)],
+                rhs=k_codes[:].bitcast(FP4X4),
+                rhs_scale=k_scales[:],
+                start=True,
+                stop=True,
+            )
+        p_t = turns.tile([P, PACK, I], F32, name="p_t", offset=14336, align_bytes=64)
+        w_flat = keep.tile([P, PACK, I], BF16, name="w_flat")
+        for b in range(2):
+            nmax = keep.tile([P, 2], F32, name=f"nmax{b}")
+            nc.vector.tensor_reduce(nmax[:], score[b][:], AX.X, ALU.max, negate=True)
+            sums = keep.tile([P, 2], F32, name=f"sums{b}")
+            for k in range(2):
+                nc.scalar.activation(p_t[:, 2 * b + k, :], score[b][:, k, :], ACT.Exp, bias=nmax[:, k : k + 1], accum_out=sums[:, k : k + 1])
+            inv = keep.tile([P, 2], F32, name=f"inv{b}")
+            nc.vector.reciprocal(inv[:], sums[:])
+            rs = keep.tile([P, 2], F32, name=f"rs{b}")
+            nc.vector.tensor_tensor(rs[:], inv[:], qs_cols[:, 2 * b : 2 * b + 2], ALU.mult)
+            for k in range(2):
+                nc.scalar.activation(w_flat[:, 2 * b + k, :], p_t[:, 2 * b + k, :], ACT.Copy, scale=rs[:, k : k + 1])
+
+        g_codes = keep.tile([P, E], U32, name="g_codes", align_bytes=64)
+        g_scales = keep.tile([P, E], U8, name="g_scales", align_bytes=64)
+
+        def prep_grows(h):
+            g_woven = turns.tile([P, E // 2, PACK], BF16, name=f"g_woven{h}", offset=(18432, 14336)[h], align_bytes=64)
+            nc.scalar.copy(g_woven[:].rearrange("p (c i) r -> p c r i", i=4), g_raw[h][:].rearrange("p r (c i) -> p c r i", i=4))
+            nc.vector.quantize_mx(
+                out=g_codes[:, 256 * h : 256 * h + 256].bitcast(FP8X4),
+                scales=g_scales[:, 256 * h : 256 * h + 256],
+                in_=g_woven[:].rearrange("p e r -> p (e r)"),
+            )
+
+        sq = [keep.tile([P, I], F32, name=f"sq{j}") for j in range(NE)]
+
+        def forward(j):
+            x1 = turns.tile([P, I], F32, name=f"x1_{j}", offset=(3072, 4096, 8192, 9216)[j], align_bytes=64)
+            nc.vector.tensor_tensor(x1[:], v_pool[j][:].indirect(offsets[:]), pre_row[:], ALU.mult)
+            s1 = work.tile([P, G], F32, name="s1")
+            x1p = x1[:].rearrange("p (g k) -> p g k", k=PAGE)
+            nc.vector.tensor_reduce(s1[:], x1p, AX.X, ALU.add)
+            x2 = work.tile([P, G, PAGE], F32, name="x2")
+            nc.vector.scalar_tensor_tensor(x2[:], s1[:].unsqueeze(2).to_broadcast([P, G, PAGE]), nshare[:, j : j + 1], x1p, ALU.mult, ALU.add)
+            vp = work.tile([P, I], F32, name="vp")
+            nc.scalar.activation(vp[:], x2[:].rearrange("p g k -> p (g k)"), ACT.Tanh)
+            nc.scalar.activation(sq[j][:], vp[:], ACT.Square)
+
+        prep_grows(0)
+        forward(0)
+
+        w_woven = turns.tile([P, I, PACK], BF16, name="w_woven", offset=8192, align_bytes=64)
+        nc.vector.tensor_copy(w_woven[:].rearrange("p (c i) r -> p c r i", i=4), w_flat[:].rearrange("p r (c i) -> p c r i", i=4))
+        w_codes = keep.tile([P, I], U32, name="w_codes", align_bytes=64)
+        w_scales = keep.tile([P, I], U8, name="w_scales", align_bytes=64)
+        nc.vector.quantize_mx(out=w_codes[:].bitcast(FP8X4), scales=w_scales[:], in_=w_woven[:].rearrange("p i r -> p (i r)"))
+
+        forward(1)
+
+        spread = psum.tile([P, 2, P], F32, name="sg_spread", offset=BANK["s0"])
+        for c in range(2):
+            nc.tensor.transpose(spread[:, c, :], slot_cols[1][:, c : c + 1].to_broadcast([P, P]), ident[:])
+        nc.scalar.activation(nsg_row[:].rearrange("p (n c) -> p n c", c=2), spread[:].rearrange("p c n -> p n c"), ACT.Copy, scale=-1.0)
+        turn = psum.tile([P, 512], F32, name="turn0", offset=BANK["s1"])
+        nc.tensor.transpose(turn[:, 0:P], rows[:], ident[:])
+        cols = keep.tile([P, NB], F32, name="cols")
+        nc.scalar.copy(cols[:], turn[:, 0:NB])
+
+        for c in range(4):
+            if c % 2 == 0:
+                old_raw[c] = ring.tile([P, NE, 256], F32, name=f"old_raw{c}", offset=4096 * (3 + c // 2))
+            else:
+                old_raw[c] = turns.tile([P, NE, 256], F32, name=f"old_raw{c}", offset=4096 * (c // 2), align_bytes=64)
+            nc.sync.dma_start(old_raw[c][:], old.rearrange("(j p) t -> p j t", p=P)[:, :, 256 * c : 256 * c + 256])
+
+        c0 = [psum.tile([P, 2, I], F32, name=f"c0_{b}", offset=BANK[f"c{b}"]) for b in range(2)]
+
+        def product(j):
+            nc.tensor.matmul_mx(
+                out=c0[j // 2][:, j % 2, :],
+                lhsT=g_codes[:, P * j : P * (j + 1)].bitcast(FP8X4),
+                lhsT_scale=g_scales[:, P * j : P * (j + 1)],
+                rhs=w_codes[:].bitcast(FP8X4),
+                rhs_scale=w_scales[:],
+                start=True,
+                stop=True,
+            )
+
+        faded = [keep.tile([P, E], F32, name=f"faded{b}") for b in range(NB)]
+
+        def fade_block(b):
+            turned = psum.tile([P, E], F32, name=f"turned{b}", offset=BANK[f"x{b % 2}"])
+            for j in range(NE):
+                nc.tensor.transpose(turned[:, P * j : P * (j + 1)], old_raw[b // 2][:, j, P * (b % 2) : P * (b % 2 + 1)], ident[:])
+            nc.scalar.activation(faded[b][:], turned[:], ACT.Copy, scale=cols[:, b : b + 1])
+
+        def backward(j):
+            ndx2 = work.tile([P, I], F32, name="ndx2")
+            nc.vector.scalar_tensor_tensor(ndx2[:], sq[j][:], 1.0, c0[j // 2][:, j % 2, :], ALU.subtract, ALU.mult)
+            s2 = work.tile([P, G], F32, name="s2")
+            np_ = ndx2[:].rearrange("p (g k) -> p g k", k=PAGE)
+            nc.vector.tensor_reduce(s2[:], np_, AX.X, ALU.add)
+            ndx1 = turns.tile([P, I], F32, name=f"ndx1_{j}", offset=10240 + 1024 * j, align_bytes=64)
+            nc.vector.scalar_tensor_tensor(ndx1[:].rearrange("p (g k) -> p g k", k=PAGE), s2[:].unsqueeze(2).to_broadcast([P, G, PAGE]), nshare[:, j : j + 1], np_, ALU.mult, ALU.add)
+            nc.vector.tensor_tensor(gf[j][:].indirect(offsets[:]), ndx1[:], nsg_row[:], ALU.mult)
+
+        def store(j, u, res):
+            nc.sync.dma_start(out[P * j : P * (j + 1), 512 * u : 512 * u + 512], res[:])
+
+        def turn_back(j, u, tag):
+            back = psum.tile([P, 512], F32, name=f"back{j}_{u}", offset=BANK[tag])
+            for k in range(4):
+                nc.tensor.transpose(back[:, P * k : P * (k + 1)], faded[4 * u + k][:, P * j : P * (j + 1)], ident[:])
+            return back
+
+        def finish_v(j, u, back):
+            res = outp.tile([P, 512], F32, name="res")
+            nc.vector.tensor_tensor(res[:], back[:], gf[j][:, 512 * u : 512 * u + 512], ALU.add)
+            store(j, u, res)
+
+        def turn_gf(j, u, tag):
+            bank = psum.tile([P, 512], F32, name=f"gft{j}_{u}", offset=BANK[tag])
+            for k in range(4):
+                nc.tensor.transpose(bank[:, P * k : P * (k + 1)], gf[j][:, 512 * u + P * k : 512 * u + P * (k + 1)], ident[:])
+            gft = turns.tile([P, 512], F32, name=f"gft_sb{j}_{u}", offset=24576 + 2048 * u, align_bytes=64)
+            nc.scalar.copy(gft[:], bank[:])
+            return gft
+
+        def finish_t(j, u, gft, tag):
+            back = psum.tile([P, 512], F32, name=f"back{j}_{u}", offset=BANK[tag])
+            for k in range(4):
+                nc.tensor.matmul(back[:, P * k : P * (k + 1)], faded[4 * u + k][:, P * j : P * (j + 1)], ident[:], start=True, stop=False, is_transpose=True)
+                nc.tensor.matmul(back[:, P * k : P * (k + 1)], gft[:, P * k : P * (k + 1)], ident[:], start=False, stop=True, is_transpose=True)
+            res = outp.tile([P, 512], F32, name="res")
+            nc.scalar.copy(res[:], back[:])
+            store(j, u, res)
+
+        product(0)
+        product(1)
+        forward(2)
+        prep_grows(1)
+        forward(3)
+        product(2)
+        product(3)
+        for b in range(NB):
+            fade_block(b)
+        for j in range(NE):
+            backward(j)
+        backs = {(2, 1): turn_back(2, 1, "s0"), (3, 0): turn_back(3, 0, "s1"), (3, 1): turn_back(3, 1, "c0")}
+        for j in range(2):
+            first, second = ("x", "y") if j == 0 else ("y", "x")
+            turned_halves = [turn_gf(j, u, f"{first}{u}") for u in range(2)]
+            for u in range(2):
+                finish_t(j, u, turned_halves[u], f"{second}{u}")
+        finish_t(2, 0, turn_gf(2, 0, "x0"), "y0")
+        for (j, u), back in backs.items():
+            finish_v(j, u, back)

@@ -51,21 +51,18 @@ def tile_attend_bvpagecentred_s_kernel(tc, query, qs, grows, vals, keys_words, k
         nc.scalar.activation(warm_out[:], warm[:], ACT.Exp)
 
         slot_cols = [turns.tile([P, 2], F32, name="pre_cols", offset=18432, align_bytes=64), keep.tile([P, 2], F32, name="sg_cols")]
-        share_cols = keep.tile([P, NE], F32, name="share_cols")
         qs_cols = keep.tile([P, PACK], F32, name="qs_cols")
-        q_raw = [ring.tile([P, PACK, Q // 2], F32, name=f"q_raw{h}", offset=4096 * h) for h in range(2)]
-
-        def load_query(h):
-            nc.sync.dma_start(q_raw[h][:], query.rearrange("(p j) q -> p j q", j=PACK)[:, :, 256 * h : 256 * h + 256])
+        q_raw = ring.tile([P, PACK, Q], F32, name="q_raw", offset=0)
 
         nc.sync.dma_start(offsets[:], offs)
         nc.sync.dma_start(slot_cols[0][:], pre.rearrange("o (p c) -> p (o c)", c=2))
-        load_query(0)
         nc.sync.dma_start(key_words[:].bitcast(I32), keys_words[0].bitcast(I32))
-        load_query(1)
+        nc.sync.dma_start(q_raw[:], query.rearrange("(p j) q -> p j q", j=PACK))
         for quad in range(4):
             nc.scalar.dma_start(key_scales[32 * quad : 32 * quad + 4, :].bitcast(I32), keys_scales[0, 4 * quad : 4 * quad + 4, :].bitcast(I32))
-        nc.sync.dma_start(share_cols[:], share.rearrange("(j p) o -> p (j o)", p=P), allow_slow_non_contiguous=True)
+        nc.sync.dma_start(rows[0:8, :], fade.rearrange("o (b p) -> (o b) p", p=P))
+        nc.sync.dma_start(rows[8:12, :], share.rearrange("(j p) o -> j (p o)", p=P))
+        nc.sync.dma_start(slot_cols[1][:], sg.rearrange("o (p c) -> p (o c)", c=2))
         nc.sync.dma_start(qs_cols[:], qs.rearrange("(p r) o -> p (r o)", r=PACK))
 
         v_pool, g_raw, old_raw = {}, {}, {}
@@ -80,8 +77,6 @@ def tile_attend_bvpagecentred_s_kernel(tc, query, qs, grows, vals, keys_words, k
 
         load_grows(0)
         load_vals(0)
-        nc.sync.dma_start(slot_cols[1][:], sg.rearrange("o (p c) -> p (o c)", c=2))
-        nc.sync.dma_start(rows[0:8, :], fade.rearrange("o (b p) -> (o b) p", p=P))
         load_vals(1)
         load_vals(2)
         load_vals(3)
@@ -92,8 +87,6 @@ def tile_attend_bvpagecentred_s_kernel(tc, query, qs, grows, vals, keys_words, k
             gf[j] = keep.tile([P, T], F32, name=f"gf{j}")
             nc.vector.memset(gf[j][:], 0.0)
 
-        nshare = keep.tile([P, NE], F32, name="nshare")
-        nc.gpsimd.tensor_scalar(nshare[:], share_cols[:], -1.0 / PAGE, 0.0, ALU.mult, ALU.add)
         pre_row = keep.tile([P, I], F32, name="pre_row")
         nsg_row = keep.tile([P, I], F32, name="nsg_row")
         for c in range(2):
@@ -108,17 +101,27 @@ def tile_attend_bvpagecentred_s_kernel(tc, query, qs, grows, vals, keys_words, k
 
         q_woven = turns.tile([P, PACK, P, PACK], BF16, name="q_woven", offset=18432, align_bytes=64)
 
-        def weave_q(eng, h, s0, s1):
-            dst = q_woven[:, :, 64 * h + s0 : 64 * h + s1, :].rearrange("p r s j -> p s j r")
-            src = q_raw[h][:, :, 4 * s0 : 4 * s1].rearrange("p j (s r) -> p s j r", r=PACK)
+        def weave_q(eng, s0, s1):
+            dst = q_woven[:, :, s0:s1, :].rearrange("p r s j -> p s j r")
+            src = q_raw[:, :, 4 * s0 : 4 * s1].rearrange("p j (s r) -> p s j r", r=PACK)
             if eng == "v":
                 nc.vector.tensor_copy(dst, src)
             else:
                 nc.scalar.copy(dst, src)
 
-        weave_q("v", 0, 0, 64)
-        weave_q("v", 1, 0, 40)
-        weave_q("s", 1, 40, 64)
+        weave_q("v", 0, 84)
+        weave_q("s", 84, 128)
+        spread = psum.tile([P, 2, P], F32, name="sg_spread", offset=BANK["x1"])
+        for c in range(2):
+            nc.tensor.transpose(spread[:, c, :], slot_cols[1][:, c : c + 1].to_broadcast([P, P]), ident[:])
+        nc.scalar.activation(nsg_row[:].rearrange("p (n c) -> p n c", c=2), spread[:].rearrange("p c n -> p n c"), ACT.Copy, scale=-1.0)
+        turn = psum.tile([P, 512], F32, name="turn0", offset=BANK["x0"])
+        nc.tensor.transpose(turn[:, 0:P], rows[:], ident[:])
+        cols = keep.tile([P, NB], F32, name="cols")
+        nc.scalar.copy(cols[:], turn[:, 0:NB])
+        nshare = keep.tile([P, NE], F32, name="nshare")
+        nc.scalar.activation(nshare[:], turn[:, NB : NB + NE], ACT.Copy, scale=-1.0 / PAGE)
+
         q_codes = turns.tile([P, Q], U32, name="q_codes", offset=3072, align_bytes=64)
         q_scales = keep.tile([P, Q], U8, name="q_scales", align_bytes=64)
         for b in range(2):
@@ -192,21 +195,10 @@ def tile_attend_bvpagecentred_s_kernel(tc, query, qs, grows, vals, keys_words, k
 
         forward(1)
 
-        spread = psum.tile([P, 2, P], F32, name="sg_spread", offset=BANK["s0"])
-        for c in range(2):
-            nc.tensor.transpose(spread[:, c, :], slot_cols[1][:, c : c + 1].to_broadcast([P, P]), ident[:])
-        nc.scalar.activation(nsg_row[:].rearrange("p (n c) -> p n c", c=2), spread[:].rearrange("p c n -> p n c"), ACT.Copy, scale=-1.0)
-        turn = psum.tile([P, 512], F32, name="turn0", offset=BANK["s1"])
-        nc.tensor.transpose(turn[:, 0:P], rows[:], ident[:])
-        cols = keep.tile([P, NB], F32, name="cols")
-        nc.scalar.copy(cols[:], turn[:, 0:NB])
-
-        for c in range(4):
-            if c % 2 == 0:
-                old_raw[c] = ring.tile([P, NE, 256], F32, name=f"old_raw{c}", offset=4096 * (3 + c // 2))
-            else:
-                old_raw[c] = turns.tile([P, NE, 256], F32, name=f"old_raw{c}", offset=4096 * (c // 2), align_bytes=64)
-            nc.sync.dma_start(old_raw[c][:], old.rearrange("(j p) t -> p j t", p=P)[:, :, 256 * c : 256 * c + 256])
+        old_raw[0] = ring.tile([P, NE, 512], F32, name="old_raw0", offset=4096 * 3)
+        old_raw[1] = turns.tile([P, NE, 512], F32, name="old_raw1", offset=0, align_bytes=64)
+        for u in range(2):
+            nc.sync.dma_start(old_raw[u][:], old.rearrange("(j p) t -> p j t", p=P)[:, :, 512 * u : 512 * u + 512])
 
         c0 = [psum.tile([P, 2, I], F32, name=f"c0_{b}", offset=BANK[f"c{b}"]) for b in range(2)]
 
@@ -226,7 +218,7 @@ def tile_attend_bvpagecentred_s_kernel(tc, query, qs, grows, vals, keys_words, k
         def fade_block(b):
             turned = psum.tile([P, E], F32, name=f"turned{b}", offset=BANK[f"x{b % 2}"])
             for j in range(NE):
-                nc.tensor.transpose(turned[:, P * j : P * (j + 1)], old_raw[b // 2][:, j, P * (b % 2) : P * (b % 2 + 1)], ident[:])
+                nc.tensor.transpose(turned[:, P * j : P * (j + 1)], old_raw[b // 4][:, j, P * (b % 4) : P * (b % 4 + 1)], ident[:])
             nc.scalar.activation(faded[b][:], turned[:], ACT.Copy, scale=cols[:, b : b + 1])
 
         def backward(j):
@@ -268,7 +260,7 @@ def tile_attend_bvpagecentred_s_kernel(tc, query, qs, grows, vals, keys_words, k
                 nc.tensor.matmul(back[:, P * k : P * (k + 1)], gft[:, P * k : P * (k + 1)], ident[:], start=False, stop=True, is_transpose=True)
             res = outp.tile([P, 512], F32, name="res")
             nc.scalar.copy(res[:], back[:])
-            store(j, u, res)
+            nc.scalar.dma_start(out[P * j : P * (j + 1), 512 * u : 512 * u + 512], res[:])
 
         product(0)
         product(1)
@@ -279,14 +271,19 @@ def tile_attend_bvpagecentred_s_kernel(tc, query, qs, grows, vals, keys_words, k
         product(3)
         for b in range(NB):
             fade_block(b)
-        for j in range(NE):
-            backward(j)
-        backs = {(2, 1): turn_back(2, 1, "s0"), (3, 0): turn_back(3, 0, "s1"), (3, 1): turn_back(3, 1, "c0")}
+        backward(0)
+        backward(1)
+        backs = {(2, u): turn_back(2, u, f"s{u}") for u in range(2)}
+        backward(2)
+        for u in range(2):
+            finish_v(2, u, backs[2, u])
+        backward(3)
+        backs[3, 0] = turn_back(3, 0, "c0")
         for j in range(2):
-            first, second = ("x", "y") if j == 0 else ("y", "x")
-            turned_halves = [turn_gf(j, u, f"{first}{u}") for u in range(2)]
+            turned_halves = [turn_gf(j, u, f"x{u}") for u in range(2)]
             for u in range(2):
-                finish_t(j, u, turned_halves[u], f"{second}{u}")
-        finish_t(2, 0, turn_gf(2, 0, "x0"), "y0")
-        for (j, u), back in backs.items():
-            finish_v(j, u, back)
+                finish_t(j, u, turned_halves[u], f"y{u}")
+            if j == 0:
+                backs[3, 1] = turn_back(3, 1, "c1")
+        for u in range(2):
+            finish_v(3, u, backs[3, u])

@@ -30,7 +30,7 @@ def tile_attend_bvpagecentred_s_kernel(tc, query, qs, grows, vals, keys_words, k
     nc = tc.nc
     with ExitStack() as ctx:
         keep = ctx.enter_context(tc.tile_pool(name="keep", bufs=1))
-        work = ctx.enter_context(tc.tile_pool(name="work", bufs=2))
+        work = ctx.enter_context(tc.tile_pool(name="work", bufs=4))
         outp = ctx.enter_context(tc.tile_pool(name="outp", bufs=8))
         ring = ctx.enter_context(tc.tile_pool(name="ring", bufs=1))
         turns = ctx.enter_context(tc.tile_pool(name="turns", bufs=1))
@@ -68,23 +68,23 @@ def tile_attend_bvpagecentred_s_kernel(tc, query, qs, grows, vals, keys_words, k
         v_pool, g_raw, old_raw = {}, {}, {}
 
         def load_vals(j):
-            v_pool[j] = ring.tile([P, T], F32, name=f"v_pool{j}", offset=4096 * (3, 4, 0, 1)[j])
+            v_pool[j] = ring.tile([P, T], F32, name=f"v_pool{j}", offset=4096 * (3, 4, 5, 2)[j], align_bytes=64)
             nc.sync.dma_start(v_pool[j][:], vals[P * j : P * (j + 1), :])
 
         def load_grows(h):
-            g_raw[h] = ring.tile([P, PACK, E // 2], F32, name=f"g_raw{h}", offset=4096 * 2)
+            if h == 0:
+                g_raw[h] = ring.tile([P, PACK, E // 2], F32, name="g_raw0", offset=4096 * 2)
+            else:
+                g_raw[h] = turns.tile([P, PACK, E // 2], F32, name="g_raw1", offset=14336, align_bytes=64)
             nc.sync.dma_start(g_raw[h][:], grows.rearrange("(p r) e -> p r e", r=PACK)[:, :, 256 * h : 256 * h + 256])
 
         load_grows(0)
         load_vals(0)
         load_vals(1)
-        load_vals(2)
-        load_vals(3)
-        load_grows(1)
 
         gf = {}
         for j in (0, 1, 3):
-            gf[j] = keep.tile([P, T], F32, name=f"gf{j}")
+            gf[j] = turns.tile([P, T], F32, name=f"gf{j}", offset=24576 + 4096 * j, align_bytes=64)
             nc.vector.memset(gf[j][:], 0.0)
 
         pre_row = keep.tile([P, I], F32, name="pre_row")
@@ -123,7 +123,7 @@ def tile_attend_bvpagecentred_s_kernel(tc, query, qs, grows, vals, keys_words, k
         nc.scalar.activation(nshare[:], turn[:, NB : NB + NE], ACT.Copy, scale=-1.0 / PAGE)
 
         q_codes = turns.tile([P, Q], U32, name="q_codes", offset=3072, align_bytes=64)
-        q_scales = keep.tile([P, Q], U8, name="q_scales", align_bytes=64)
+        q_scales = ring.tile([P, Q], U8, name="q_scales", offset=4096 * 5, align_bytes=64)
         for b in range(2):
             nc.vector.quantize_mx(
                 out=q_codes[:, 256 * b : 256 * b + 256].bitcast(FP8X4),
@@ -162,7 +162,7 @@ def tile_attend_bvpagecentred_s_kernel(tc, query, qs, grows, vals, keys_words, k
         g_scales = keep.tile([P, E], U8, name="g_scales", align_bytes=64)
 
         def prep_grows(h):
-            g_woven = turns.tile([P, E // 2, PACK], BF16, name=f"g_woven{h}", offset=(18432, 14336)[h], align_bytes=64)
+            g_woven = turns.tile([P, E // 2, PACK], BF16, name=f"g_woven{h}", offset=(18432, 18432)[h], align_bytes=64)
             nc.scalar.copy(g_woven[:].rearrange("p (c i) r -> p c r i", i=4), g_raw[h][:].rearrange("p r (c i) -> p c r i", i=4))
             nc.vector.quantize_mx(
                 out=g_codes[:, 256 * h : 256 * h + 256].bitcast(FP8X4),
@@ -170,7 +170,7 @@ def tile_attend_bvpagecentred_s_kernel(tc, query, qs, grows, vals, keys_words, k
                 in_=g_woven[:].rearrange("p e r -> p (e r)"),
             )
 
-        sq = [keep.tile([P, I], F32, name=f"sq{j}") for j in range(NE)]
+        sq = [turns.tile([P, I], F32, name=f"sq{j}", offset=10240 + 1024 * j, align_bytes=64) for j in range(NE)]
 
         def forward(j):
             x1 = turns.tile([P, I], F32, name=f"x1_{j}", offset=(3072, 4096, 8192, 9216)[j], align_bytes=64)
@@ -178,10 +178,16 @@ def tile_attend_bvpagecentred_s_kernel(tc, query, qs, grows, vals, keys_words, k
             s1 = work.tile([P, G], F32, name="s1")
             x1p = x1[:].rearrange("p (g k) -> p g k", k=PAGE)
             nc.vector.tensor_reduce(s1[:], x1p, AX.X, ALU.add)
-            x2 = work.tile([P, G, PAGE], F32, name="x2")
-            nc.vector.scalar_tensor_tensor(x2[:], s1[:].unsqueeze(2).to_broadcast([P, G, PAGE]), nshare[:, j : j + 1], x1p, ALU.mult, ALU.add)
             vp = work.tile([P, I], F32, name="vp")
-            nc.scalar.activation(vp[:], x2[:].rearrange("p g k -> p (g k)"), ACT.Tanh)
+            if True:
+                x2 = work.tile([P, G, PAGE], F32, name="x2")
+                nc.vector.scalar_tensor_tensor(x2[:], s1[:].unsqueeze(2).to_broadcast([P, G, PAGE]), nshare[:, j : j + 1], x1p, ALU.mult, ALU.add)
+                nc.scalar.activation(vp[:], x2[:].rearrange("p g k -> p (g k)"), ACT.Tanh)
+            else:
+                off = work.tile([P, G], F32, name="off")
+                nc.scalar.activation(off[:], s1[:], ACT.Copy, scale=nshare[:, j : j + 1])
+                for g in range(G):
+                    nc.scalar.activation(vp[:, PAGE * g : PAGE * (g + 1)], x1[:, PAGE * g : PAGE * (g + 1)], ACT.Tanh, bias=off[:, g : g + 1])
             nc.scalar.activation(sq[j][:], vp[:], ACT.Square)
 
         prep_grows(0)
@@ -195,10 +201,17 @@ def tile_attend_bvpagecentred_s_kernel(tc, query, qs, grows, vals, keys_words, k
 
         forward(1)
 
-        old_raw[0] = ring.tile([P, NE, 512], F32, name="old_raw0", offset=4096 * 3)
+        old_raw[0] = ring.tile([P, NE, 512], F32, name="old_raw0", offset=0)
         old_raw[1] = turns.tile([P, NE, 512], F32, name="old_raw1", offset=0, align_bytes=64)
-        for u in range(2):
+
+        def load_old(u):
             nc.sync.dma_start(old_raw[u][:], old.rearrange("(j p) t -> p j t", p=P)[:, :, 512 * u : 512 * u + 512])
+
+        load_old(0)
+        load_vals(2)
+        load_vals(3)
+        load_grows(1)
+        load_old(1)
 
         c0 = [psum.tile([P, 2, I], F32, name=f"c0_{b}", offset=BANK[f"c{b}"]) for b in range(2)]
 
@@ -221,14 +234,20 @@ def tile_attend_bvpagecentred_s_kernel(tc, query, qs, grows, vals, keys_words, k
                 nc.tensor.transpose(turned[:, P * j : P * (j + 1)], old_raw[b // 4][:, j, P * (b % 4) : P * (b % 4 + 1)], ident[:])
             nc.scalar.activation(faded[b][:], turned[:], ACT.Copy, scale=cols[:, b : b + 1])
 
-        def backward(j):
+        ndx2s = {}
+
+        def page_sums(j):
             ndx2 = work.tile([P, I], F32, name="ndx2")
             nc.vector.scalar_tensor_tensor(ndx2[:], sq[j][:], 1.0, c0[j // 2][:, j % 2, :], ALU.subtract, ALU.mult)
             s2 = work.tile([P, G], F32, name="s2")
             np_ = ndx2[:].rearrange("p (g k) -> p g k", k=PAGE)
             nc.vector.tensor_reduce(s2[:], np_, AX.X, ALU.add)
-            ndx1 = turns.tile([P, I], F32, name=f"ndx1_{j}", offset=10240 + 1024 * j, align_bytes=64)
-            nc.vector.scalar_tensor_tensor(ndx1[:].rearrange("p (g k) -> p g k", k=PAGE), s2[:].unsqueeze(2).to_broadcast([P, G, PAGE]), nshare[:, j : j + 1], np_, ALU.mult, ALU.add)
+            ndx2s[j] = (ndx2, s2)
+
+        def backward(j):
+            ndx2, s2 = ndx2s[j]
+            ndx1 = turns.tile([P, I], F32, name=f"ndx1_{j}", offset=(40960, 41984, 24576, 28672)[j], align_bytes=64)
+            nc.vector.scalar_tensor_tensor(ndx1[:].rearrange("p (g k) -> p g k", k=PAGE), s2[:].unsqueeze(2).to_broadcast([P, G, PAGE]), nshare[:, j : j + 1], ndx2[:].rearrange("p (g k) -> p g k", k=PAGE), ALU.mult, ALU.add)
             nc.vector.tensor_tensor(gf[j][:].indirect(offsets[:]), ndx1[:], nsg_row[:], ALU.mult)
 
         def store(j, u, res):
@@ -271,19 +290,11 @@ def tile_attend_bvpagecentred_s_kernel(tc, query, qs, grows, vals, keys_words, k
         product(3)
         for b in range(NB):
             fade_block(b)
-        backward(0)
-        backward(1)
-        backs = {(2, u): turn_back(2, u, f"s{u}") for u in range(2)}
-        backward(2)
-        for u in range(2):
-            finish_v(2, u, backs[2, u])
-        backward(3)
-        backs[3, 0] = turn_back(3, 0, "c0")
-        for j in range(2):
-            turned_halves = [turn_gf(j, u, f"x{u}") for u in range(2)]
+        page_sums(0)
+        for j in range(NE):
+            if j + 1 < NE:
+                page_sums(j + 1)
+            backs = [turn_back(j, u, f"{'ys'[j % 2]}{u}") for u in range(2)]
+            backward(j)
             for u in range(2):
-                finish_t(j, u, turned_halves[u], f"y{u}")
-            if j == 0:
-                backs[3, 1] = turn_back(3, 1, "c1")
-        for u in range(2):
-            finish_v(3, u, backs[3, u])
+                finish_v(j, u, backs[u])

from contextlib import ExitStack

import concourse.mybir as mybir
from concourse.masks import make_identity

D, E, T, I, Q, G = 512, 512, 1024, 256, 512, 16
FLOPS = 2 * D * Q * I + 2 * Q * E * I

F32 = mybir.dt.float32
BF16 = mybir.dt.bfloat16
I32 = mybir.dt.int32
U32 = mybir.dt.uint32
U16 = mybir.dt.uint16
U8 = mybir.dt.uint8
FP8X4 = mybir.dt.float8_e4m3fn_x4
FP4X4 = mybir.dt.float4_e2m1fn_x4
ALU = mybir.AluOpType
ACT = mybir.ActivationFunctionType
AX = mybir.AxisListType

P = 128
PACK = 4
PAGE = I // G
NE = E // P
NB = T // P
BANK = {name: 2048 * n for n, name in enumerate(("s0", "s1", "c0", "c1", "x0", "x1", "y0", "y1"))}


def tile_attend_bvpagecentred_s_kernel(tc, query, qs, grows, vals, keys_words, keys_scales, share, pre, sg, old, fade, offs, out):
    nc = tc.nc
    with ExitStack() as ctx:
        keep = ctx.enter_context(tc.tile_pool(name="keep", bufs=1))
        work = ctx.enter_context(tc.tile_pool(name="work", bufs=4))
        outp = ctx.enter_context(tc.tile_pool(name="outp", bufs=8))
        ring = ctx.enter_context(tc.tile_pool(name="ring", bufs=1))
        turns = ctx.enter_context(tc.tile_pool(name="turns", bufs=1))
        psum = ctx.enter_context(tc.psum_pool(name="psum", bufs=1))

        offsets = keep.tile([P, I // 16], U16, name="offsets")
        key_words = keep.tile([P, T], U16, name="key_words")
        key_scales = keep.tile([P, T], U8, name="key_scales")
        rows = keep.tile([P, P], F32, name="rows")
        ident = keep.tile([P, P], F32, name="ident")
        warm = keep.tile([P, 1], F32, name="warm")
        warm_out = keep.tile([P, 1], F32, name="warm_out")

        nc.gpsimd.memset(rows[:], 0.0)
        make_identity(nc, ident[:])
        nc.vector.memset(key_scales[:].bitcast(I32), 0)
        nc.vector.memset(warm[:], 0.0)
        nc.scalar.activation(warm_out[:], warm[:], ACT.Exp)

        slot_cols = [turns.tile([P, 2], F32, name="pre_cols", offset=18432, align_bytes=64), keep.tile([P, 2], F32, name="sg_cols")]
        qs_cols = keep.tile([P, PACK], F32, name="qs_cols")
        q_raw = ring.tile([P, PACK, Q], F32, name="q_raw", offset=0)

        nc.sync.dma_start(offsets[:], offs)
        nc.sync.dma_start(slot_cols[0][:], pre.rearrange("o (p c) -> p (o c)", c=2))
        nc.sync.dma_start(key_words[:].bitcast(I32), keys_words[0].bitcast(I32))
        nc.sync.dma_start(q_raw[:], query.rearrange("(p j) q -> p j q", j=PACK))
        for quad in range(4):
            nc.scalar.dma_start(key_scales[32 * quad : 32 * quad + 4, :].bitcast(I32), keys_scales[0, 4 * quad : 4 * quad + 4, :].bitcast(I32))
        nc.sync.dma_start(rows[0:8, :], fade.rearrange("o (b p) -> (o b) p", p=P))
        nc.sync.dma_start(rows[8:12, :], share.rearrange("(j p) o -> j (p o)", p=P))
        nc.sync.dma_start(slot_cols[1][:], sg.rearrange("o (p c) -> p (o c)", c=2))
        nc.sync.dma_start(qs_cols[:], qs.rearrange("(p r) o -> p (r o)", r=PACK))

        v_pool, g_raw, old_raw = {}, {}, {}

        def load_vals(j):
            v_pool[j] = ring.tile([P, T], F32, name=f"v_pool{j}", offset=4096 * (3, 4, 5, 2)[j], align_bytes=64)
            nc.sync.dma_start(v_pool[j][:], vals[P * j : P * (j + 1), :])

        def load_grows(h):
            if h == 0:
                g_raw[h] = ring.tile([P, PACK, E // 2], F32, name="g_raw0", offset=4096 * 2)
            else:
                g_raw[h] = turns.tile([P, PACK, E // 2], F32, name="g_raw1", offset=14336, align_bytes=64)
            nc.sync.dma_start(g_raw[h][:], grows.rearrange("(p r) e -> p r e", r=PACK)[:, :, 256 * h : 256 * h + 256])

        load_grows(0)
        load_vals(0)
        load_vals(1)

        gf = {}
        for j in (0, 1, 3):
            gf[j] = turns.tile([P, T], F32, name=f"gf{j}", offset=24576 + 4096 * j, align_bytes=64)
            nc.vector.memset(gf[j][:], 0.0)

        pre_row = keep.tile([P, I], F32, name="pre_row")
        nsg_row = keep.tile([P, I], F32, name="nsg_row")
        for c in range(2):
            spread = psum.tile([P, P], F32, name=f"pre_spread{c}", offset=BANK[f"s{c}"])
            nc.tensor.transpose(spread[:], slot_cols[0][:, c : c + 1].to_broadcast([P, P]), ident[:])
            nc.scalar.copy(pre_row[:, c::2], spread[:])

        k_codes = keep.tile([P, I], U16, name="k_codes", align_bytes=64)
        k_scales = keep.tile([P, I], U8, name="k_scales", align_bytes=64)
        nc.vector.tensor_copy(k_codes[:], key_words[:].indirect(offsets[:]))
        nc.vector.tensor_copy(k_scales[:], key_scales[:].indirect(offsets[:]))

        q_woven = turns.tile([P, PACK, P, PACK], BF16, name="q_woven", offset=18432, align_bytes=64)

        def weave_q(eng, s0, s1):
            dst = q_woven[:, :, s0:s1, :].rearrange("p r s j -> p s j r")
            src = q_raw[:, :, 4 * s0 : 4 * s1].rearrange("p j (s r) -> p s j r", r=PACK)
            if eng == "v":
                nc.vector.tensor_copy(dst, src)
            else:
                nc.scalar.copy(dst, src)

        weave_q("v", 0, 84)
        weave_q("s", 84, 128)
        spread = psum.tile([P, 2, P], F32, name="sg_spread", offset=BANK["x1"])
        for c in range(2):
            nc.tensor.transpose(spread[:, c, :], slot_cols[1][:, c : c + 1].to_broadcast([P, P]), ident[:])
        nc.scalar.activation(nsg_row[:].rearrange("p (n c) -> p n c", c=2), spread[:].rearrange("p c n -> p n c"), ACT.Copy, scale=-1.0)
        turn = psum.tile([P, 512], F32, name="turn0", offset=BANK["x0"])
        nc.tensor.transpose(turn[:, 0:P], rows[:], ident[:])
        cols = keep.tile([P, NB], F32, name="cols")
        nc.scalar.copy(cols[:], turn[:, 0:NB])
        nshare = keep.tile([P, NE], F32, name="nshare")
        nc.scalar.activation(nshare[:], turn[:, NB : NB + NE], ACT.Copy, scale=-1.0 / PAGE)

        q_codes = turns.tile([P, Q], U32, name="q_codes", offset=3072, align_bytes=64)
        q_scales = ring.tile([P, Q], U8, name="q_scales", offset=4096 * 5, align_bytes=64)
        for b in range(2):
            nc.vector.quantize_mx(
                out=q_codes[:, 256 * b : 256 * b + 256].bitcast(FP8X4),
                scales=q_scales[:, 256 * b : 256 * b + 256],
                in_=q_woven[:, 2 * b : 2 * b + 2, :, :].rearrange("p r s j -> p (r s j)"),
            )
        gf[2] = turns.tile([P, T], F32, name="gf2", offset=18432 + 2048, align_bytes=64)
        nc.vector.memset(gf[2][:], 0.0)
        score = [psum.tile([P, 2, I], F32, name=f"score{b}", offset=BANK[f"s{b}"]) for b in range(2)]
        for r in range(PACK):
            nc.tensor.matmul_mx(
                out=score[r // 2][:, r % 2, :],
                lhsT=q_codes[:, P * r : P * (r + 1)].bitcast(FP8X4),
                lhsT_scale=q_scales[:, P * r : P * (r + 1)],
                rhs=k_codes[:].bitcast(FP4X4),
                rhs_scale=k_scales[:],
                start=True,
                stop=True,
            )
        p_t = turns.tile([P, PACK, I], F32, name="p_t", offset=14336, align_bytes=64)
        w_flat = keep.tile([P, PACK, I], BF16, name="w_flat")
        for b in range(2):
            nmax = keep.tile([P, 2], F32, name=f"nmax{b}")
            nc.vector.tensor_reduce(nmax[:], score[b][:], AX.X, ALU.max, negate=True)
            sums = keep.tile([P, 2], F32, name=f"sums{b}")
            for k in range(2):
                nc.scalar.activation(p_t[:, 2 * b + k, :], score[b][:, k, :], ACT.Exp, bias=nmax[:, k : k + 1], accum_out=sums[:, k : k + 1])
            inv = keep.tile([P, 2], F32, name=f"inv{b}")
            nc.vector.reciprocal(inv[:], sums[:])
            rs = keep.tile([P, 2], F32, name=f"rs{b}")
            nc.vector.tensor_tensor(rs[:], inv[:], qs_cols[:, 2 * b : 2 * b + 2], ALU.mult)
            for k in range(2):
                nc.scalar.activation(w_flat[:, 2 * b + k, :], p_t[:, 2 * b + k, :], ACT.Copy, scale=rs[:, k : k + 1])

        g_codes = keep.tile([P, E], U32, name="g_codes", align_bytes=64)
        g_scales = keep.tile([P, E], U8, name="g_scales", align_bytes=64)

        def prep_grows(h):
            g_woven = turns.tile([P, E // 2, PACK], BF16, name=f"g_woven{h}", offset=(18432, 18432)[h], align_bytes=64)
            nc.scalar.copy(g_woven[:].rearrange("p (c i) r -> p c r i", i=4), g_raw[h][:].rearrange("p r (c i) -> p c r i", i=4))
            nc.vector.quantize_mx(
                out=g_codes[:, 256 * h : 256 * h + 256].bitcast(FP8X4),
                scales=g_scales[:, 256 * h : 256 * h + 256],
                in_=g_woven[:].rearrange("p e r -> p (e r)"),
            )

        sq = [turns.tile([P, I], F32, name=f"sq{j}", offset=10240 + 1024 * j, align_bytes=64) for j in range(NE)]

        def forward(j):
            x1 = turns.tile([P, I], F32, name=f"x1_{j}", offset=(3072, 4096, 8192, 9216)[j], align_bytes=64)
            nc.vector.tensor_tensor(x1[:], v_pool[j][:].indirect(offsets[:]), pre_row[:], ALU.mult)
            s1 = work.tile([P, G], F32, name="s1")
            x1p = x1[:].rearrange("p (g k) -> p g k", k=PAGE)
            nc.vector.tensor_reduce(s1[:], x1p, AX.X, ALU.add)
            vp = work.tile([P, I], F32, name="vp")
            if True:
                x2 = work.tile([P, G, PAGE], F32, name="x2")
                nc.vector.scalar_tensor_tensor(x2[:], s1[:].unsqueeze(2).to_broadcast([P, G, PAGE]), nshare[:, j : j + 1], x1p, ALU.mult, ALU.add)
                nc.scalar.activation(vp[:], x2[:].rearrange("p g k -> p (g k)"), ACT.Tanh)
            else:
                off = work.tile([P, G], F32, name="off")
                nc.scalar.activation(off[:], s1[:], ACT.Copy, scale=nshare[:, j : j + 1])
                for g in range(G):
                    nc.scalar.activation(vp[:, PAGE * g : PAGE * (g + 1)], x1[:, PAGE * g : PAGE * (g + 1)], ACT.Tanh, bias=off[:, g : g + 1])
            nc.scalar.activation(sq[j][:], vp[:], ACT.Square)

        prep_grows(0)
        forward(0)

        w_woven = turns.tile([P, I, PACK], BF16, name="w_woven", offset=8192, align_bytes=64)
        nc.vector.tensor_copy(w_woven[:].rearrange("p (c i) r -> p c r i", i=4), w_flat[:].rearrange("p r (c i) -> p c r i", i=4))
        w_codes = keep.tile([P, I], U32, name="w_codes", align_bytes=64)
        w_scales = keep.tile([P, I], U8, name="w_scales", align_bytes=64)
        nc.vector.quantize_mx(out=w_codes[:].bitcast(FP8X4), scales=w_scales[:], in_=w_woven[:].rearrange("p i r -> p (i r)"))

        forward(1)

        old_raw[0] = ring.tile([P, NE, 512], F32, name="old_raw0", offset=0)
        old_raw[1] = turns.tile([P, NE, 512], F32, name="old_raw1", offset=0, align_bytes=64)

        def load_old(u):
            nc.sync.dma_start(old_raw[u][:], old.rearrange("(j p) t -> p j t", p=P)[:, :, 512 * u : 512 * u + 512])

        load_old(0)
        load_vals(2)
        load_vals(3)
        load_grows(1)
        load_old(1)

        c0 = [psum.tile([P, 2, I], F32, name=f"c0_{b}", offset=BANK[f"c{b}"]) for b in range(2)]

        def product(j):
            nc.tensor.matmul_mx(
                out=c0[j // 2][:, j % 2, :],
                lhsT=g_codes[:, P * j : P * (j + 1)].bitcast(FP8X4),
                lhsT_scale=g_scales[:, P * j : P * (j + 1)],
                rhs=w_codes[:].bitcast(FP8X4),
                rhs_scale=w_scales[:],
                start=True,
                stop=True,
            )

        faded = [keep.tile([P, E], F32, name=f"faded{b}") for b in range(NB)]

        def fade_block(b):
            turned = psum.tile([P, E], F32, name=f"turned{b}", offset=BANK[f"x{b % 2}"])
            for j in range(NE):
                nc.tensor.transpose(turned[:, P * j : P * (j + 1)], old_raw[b // 4][:, j, P * (b % 4) : P * (b % 4 + 1)], ident[:])
            nc.scalar.activation(faded[b][:], turned[:], ACT.Copy, scale=cols[:, b : b + 1])

        ndx2s = {}

        def page_sums(j):
            ndx2 = work.tile([P, I], F32, name="ndx2")
            nc.vector.scalar_tensor_tensor(ndx2[:], sq[j][:], 1.0, c0[j // 2][:, j % 2, :], ALU.subtract, ALU.mult)
            s2 = work.tile([P, G], F32, name="s2")
            np_ = ndx2[:].rearrange("p (g k) -> p g k", k=PAGE)
            nc.vector.tensor_reduce(s2[:], np_, AX.X, ALU.add)
            ndx2s[j] = (ndx2, s2)

        def backward(j):
            ndx2, s2 = ndx2s[j]
            ndx1 = turns.tile([P, I], F32, name=f"ndx1_{j}", offset=(40960, 41984, 24576, 28672)[j], align_bytes=64)
            nc.vector.scalar_tensor_tensor(ndx1[:].rearrange("p (g k) -> p g k", k=PAGE), s2[:].unsqueeze(2).to_broadcast([P, G, PAGE]), nshare[:, j : j + 1], ndx2[:].rearrange("p (g k) -> p g k", k=PAGE), ALU.mult, ALU.add)
            nc.vector.tensor_tensor(gf[j][:].indirect(offsets[:]), ndx1[:], nsg_row[:], ALU.mult)

        def store(j, u, res):
            nc.sync.dma_start(out[P * j : P * (j + 1), 512 * u : 512 * u + 512], res[:])

        def turn_back(j, u, tag):
            back = psum.tile([P, 512], F32, name=f"back{j}_{u}", offset=BANK[tag])
            for k in range(4):
                nc.tensor.transpose(back[:, P * k : P * (k + 1)], faded[4 * u + k][:, P * j : P * (j + 1)], ident[:])
            return back

        def finish_v(j, u, back):
            res = outp.tile([P, 512], F32, name="res")
            nc.vector.tensor_tensor(res[:], back[:], gf[j][:, 512 * u : 512 * u + 512], ALU.add)
            store(j, u, res)

        def turn_gf(j, u, tag):
            bank = psum.tile([P, 512], F32, name=f"gft{j}_{u}", offset=BANK[tag])
            for k in range(4):
                nc.tensor.transpose(bank[:, P * k : P * (k + 1)], gf[j][:, 512 * u + P * k : 512 * u + P * (k + 1)], ident[:])
            gft = turns.tile([P, 512], F32, name=f"gft_sb{j}_{u}", offset=24576 + 2048 * u, align_bytes=64)
            nc.scalar.copy(gft[:], bank[:])
            return gft

        def finish_t(j, u, gft, tag):
            back = psum.tile([P, 512], F32, name=f"back{j}_{u}", offset=BANK[tag])
            for k in range(4):
                nc.tensor.matmul(back[:, P * k : P * (k + 1)], faded[4 * u + k][:, P * j : P * (j + 1)], ident[:], start=True, stop=False, is_transpose=True)
                nc.tensor.matmul(back[:, P * k : P * (k + 1)], gft[:, P * k : P * (k + 1)], ident[:], start=False, stop=True, is_transpose=True)
            res = outp.tile([P, 512], F32, name="res")
            nc.scalar.copy(res[:], back[:])
            nc.scalar.dma_start(out[P * j : P * (j + 1), 512 * u : 512 * u + 512], res[:])

        product(0)
        product(1)
        forward(2)
        prep_grows(1)
        forward(3)
        product(2)
        product(3)
        for b in range(NB):
            fade_block(b)
        page_sums(0)
        for j in range(NE):
            if j + 1 < NE:
                page_sums(j + 1)
            backs = [turn_back(j, u, f"{'ys'[j % 2]}{u}") for u in range(2)]
            backward(j)
            for u in range(2):
                finish_v(j, u, backs[u])
